import numpy as np
import ml_dtypes


def mxq(x, axis, fmt="e4m3"):
    dtype, down = {"e4m3": (ml_dtypes.float8_e4m3fn, 7), "e5m2": (ml_dtypes.float8_e5m2, 14)}[fmt]
    v = np.moveaxis(np.asarray(x, np.float32).astype(ml_dtypes.bfloat16).astype(np.float64), axis, -1)
    blocks = v.reshape(v.shape[:-1] + (-1, 32))
    amax = np.abs(blocks).max(-1, keepdims=True)
    byte = np.maximum(np.where(amax > 0, np.frexp(amax)[1] - 1 + 127, 0) - down, 1)
    scale = np.exp2(byte - 127.0)
    codes = (blocks / scale).astype(np.float32).astype(dtype).astype(np.float64)
    return np.moveaxis((codes * scale).reshape(v.shape), -1, axis)


WIDE = False


def mx_kscale(k, group=512):
    if not WIDE:
        return np.ones(k)
    levels = np.array([10, -10, 5, -5, 0])
    if group != 512:
        return np.exp2(np.random.permutation(np.resize(levels, k // group))).repeat(group)
    if k % 512:
        return np.exp2(np.random.permutation(np.resize(levels, k // 32))).repeat(32)
    a = np.empty((k // 512, 16))
    for p in range(k // 512):
        a[p, :8] = np.random.permutation(np.resize(levels, 8))
        for g in range(8):
            far = levels[np.abs(levels - a[p, g]) >= 10]
            a[p, g + 8] = far[np.random.randint(len(far))]
    return np.exp2(a.ravel()).repeat(32)


def f64(x):
    return np.asarray(x).astype(np.float64)


E2M1 = np.array([0.0, 0.5, 1.0, 1.5, 2.0, 3.0, 4.0, 6.0, -0.0, -0.5, -1.0, -1.5, -2.0, -3.0, -4.0, -6.0])


def pack_group(w):
    k, n = w.shape
    w = f64(np.asarray(w, np.float32).astype(ml_dtypes.bfloat16)).reshape(k // 32, 32, n)
    amax = np.abs(w).max(1)
    mant, ex = np.frexp(amax / 6.0)
    byte = np.clip(np.where(amax > 0, np.where(mant > 0.5, ex, ex - 1) + 127, 1), 1, 254)
    scaled = (w * np.exp2(127.0 - byte)[:, None, :]).reshape(k, n).astype(np.float32)
    c = np.ascontiguousarray(scaled.reshape(k // 4, 4, n).transpose(0, 2, 1)).astype(ml_dtypes.float4_e2m1fn).view(np.uint8) & 0xF
    return np.ascontiguousarray((c[..., 0::2] | (c[..., 1::2] << 4)).reshape(k // 4, 2 * n)), byte.astype(np.uint8)


def unpack_group(words, scales):
    p, n = words.shape[0], scales.shape[1]
    words = np.ascontiguousarray(words).reshape(p, n, 2)
    nib = np.empty((p, n, 4), np.uint8)
    nib[..., 0::2] = words & 0xF
    nib[..., 1::2] = words >> 4
    return E2M1[nib].transpose(0, 2, 1).reshape(4 * p, n) * np.repeat(np.exp2(scales.astype(np.float64) - 127.0), 32, axis=0)


def gelu(v):
    return 0.5 * v * (1.0 + np.tanh(0.7978845608028654 * (v + 0.044715 * v ** 3)))


G, D, M, N = 4, 256, 128, 512


def setup_inputs():
    n = np.random.standard_normal
    s = mx_kscale(D, 0)[:, None]
    w_ = [pack_group(w) for w in n((G, D, M)) / np.sqrt(D) / s]
    return {
        "x": (n((G, D, N)) * s).astype(np.float32),
        "w_words": np.stack([w[0] for w in w_]),
        "w_scales": np.stack([w[1] for w in w_]),
    }


def reference(x, w_words, w_scales):
    xq = mxq(f64(x), 1, "e4m3")
    y = np.stack([unpack_group(w_words[g], w_scales[g]) for g in range(G)]).transpose(0, 2, 1) @ xq
    y = gelu(y)
    return y

@@ -1,0 +1,91 @@
+from contextlib import ExitStack
+
+import concourse.mybir as mybir
+
+G, D, M, N = 4, 256, 128, 512
+FLOPS = 2 * G * D * M * N
+
+F32 = mybir.dt.float32
+BF16 = mybir.dt.bfloat16
+I32 = mybir.dt.int32
+U32 = mybir.dt.uint32
+U8 = mybir.dt.uint8
+FP8X4 = mybir.dt.float8_e4m3fn_x4
+FP4X4 = mybir.dt.float4_e2m1fn_x4
+GELU = mybir.ActivationFunctionType.Gelu_apprx_tanh
+
+P = 128
+PACK = 4
+ROWS = D // PACK
+PAIRS = G // 2
+HALF = N // 2
+VEC_EXTRA = 64
+
+
+def interleave(copy, grouped, raw, lo, hi, base):
+    copy(
+        out=grouped[:, lo - base : hi - base, :].rearrange("p (c i) t -> p c t i", i=4),
+        in_=raw[:, :, lo:hi].rearrange("p t (c i) -> p c t i", i=4),
+    )
+
+
+def tile_rows_glin_gelu_kernel(tc, x, w_words, w_scales, out):
+    nc = tc.nc
+    with ExitStack() as ctx:
+        sb = ctx.enter_context(tc.tile_pool(name="sb", bufs=1))
+        psum = ctx.enter_context(tc.psum_pool(name="psum", bufs=1))
+        ctx.enter_context(tc.manual_schedule())
+
+        raw = [sb.tile([P, PACK, N], F32, name="raw%d" % s, align_bytes=64) for s in range(PAIRS)]
+        left = [sb.tile([P, HALF, PACK], BF16, name="left%d" % s, align_bytes=64) for s in range(PAIRS)]
+        right = [sb.tile([P, HALF, PACK], BF16, name="right%d" % s, align_bytes=64) for s in range(PAIRS)]
+        x_codes = [sb.tile([P, N], U32, name="x_codes%d" % s, align_bytes=64) for s in range(PAIRS)]
+        x_scales = [sb.tile([P, N], U8, name="x_scales%d" % s, align_bytes=64) for s in range(PAIRS)]
+        w_sb = [sb.tile([P, 2 * M], U8, name="w_sb%d" % s, align_bytes=64) for s in range(PAIRS)]
+        ws_sb = sb.tile([P, PAIRS, M], U8, name="ws_sb", align_bytes=64)
+        acc = [psum.tile([M, N], F32, name="acc%d" % g) for g in range(G)]
+        y = [sb.tile([M, N], F32, name="y%d" % g, align_bytes=64) for g in range(G)]
+
+        nc.vector.memset(ws_sb[:].bitcast(I32), 0)
+        probe = sb.tile([P, 2], F32, name="probe")
+        nc.vector.memset(probe[:, 0:1], 0.0)
+
+        for s in range(PAIRS):
+            nc.sync.dma_start(out=raw[s][:], in_=x[2 * s : 2 * s + 2].rearrange("c (p t) n -> (c p) t n", t=PACK))
+            nc.sync.dma_start(
+                out=w_sb[s][:].bitcast(I32),
+                in_=w_words[2 * s : 2 * s + 2].rearrange("c p b -> (c p) b").bitcast(I32),
+            )
+        scale_rows = w_scales.rearrange("(s c) (h i) m -> c h i s m", c=2, i=4)
+        for c in range(2):
+            for h in range(2):
+                first = ROWS * c + 32 * h
+                nc.scalar.dma_start(out=ws_sb[first : first + 4].bitcast(I32), in_=scale_rows[c, h].bitcast(I32))
+        nc.scalar.activation(out=probe[:, 1:2], in_=probe[:, 0:1], func=GELU)
+
+        split = HALF + VEC_EXTRA
+        for s in range(PAIRS):
+            interleave(nc.scalar.copy, right[s], raw[s], split, N, HALF)
+            interleave(nc.vector.tensor_copy, left[s], raw[s], 0, HALF, 0)
+            interleave(nc.vector.tensor_copy, right[s], raw[s], HALF, split, HALF)
+            for grouped, lo in ((left[s], 0), (right[s], HALF)):
+                nc.vector.quantize_mx(
+                    out=x_codes[s][:, lo : lo + HALF].bitcast(FP8X4),
+                    scales=x_scales[s][:, lo : lo + HALF],
+                    in_=grouped[:].rearrange("p n t -> p (n t)"),
+                )
+            for c in range(2):
+                rows = slice(ROWS * c, ROWS * (c + 1))
+                nc.tensor.matmul_mx(
+                    out=acc[2 * s + c][:],
+                    lhsT=w_sb[s][rows, :].bitcast(FP4X4),
+                    lhsT_scale=ws_sb[rows, s, :],
+                    rhs=x_codes[s][rows, :].bitcast(FP8X4),
+                    rhs_scale=x_scales[s][rows, :],
+                    start=True,
+                    stop=True,
+                )
+
+        for g in range(G):
+            nc.scalar.activation(out=y[g][:], in_=acc[g][:], func=GELU)
+            nc.sync.dma_start(out=out[g], in_=y[g][:])

@@ -17,16 +17,9 @@ GELU = mybir.ActivationFunctionType.Gelu_apprx_tanh
 P = 128
 PACK = 4
 ROWS = D // PACK
-PAIRS = G // 2
 HALF = N // 2
+QUARTER = N // 4
 VEC_EXTRA = 64
-
-
-def interleave(copy, grouped, raw, lo, hi, base):
-    copy(
-        out=grouped[:, lo - base : hi - base, :].rearrange("p (c i) t -> p c t i", i=4),
-        in_=raw[:, :, lo:hi].rearrange("p t (c i) -> p c t i", i=4),
-    )
 
 
 def tile_rows_glin_gelu_kernel(tc, x, w_words, w_scales, out):
@@ -36,56 +29,81 @@ def tile_rows_glin_gelu_kernel(tc, x, w_words, w_scales, out):
         psum = ctx.enter_context(tc.psum_pool(name="psum", bufs=1))
         ctx.enter_context(tc.manual_schedule())
 
-        raw = [sb.tile([P, PACK, N], F32, name="raw%d" % s, align_bytes=64) for s in range(PAIRS)]
-        left = [sb.tile([P, HALF, PACK], BF16, name="left%d" % s, align_bytes=64) for s in range(PAIRS)]
-        right = [sb.tile([P, HALF, PACK], BF16, name="right%d" % s, align_bytes=64) for s in range(PAIRS)]
-        x_codes = [sb.tile([P, N], U32, name="x_codes%d" % s, align_bytes=64) for s in range(PAIRS)]
-        x_scales = [sb.tile([P, N], U8, name="x_scales%d" % s, align_bytes=64) for s in range(PAIRS)]
-        w_sb = [sb.tile([P, 2 * M], U8, name="w_sb%d" % s, align_bytes=64) for s in range(PAIRS)]
-        ws_sb = sb.tile([P, PAIRS, M], U8, name="ws_sb", align_bytes=64)
-        acc = [psum.tile([M, N], F32, name="acc%d" % g) for g in range(G)]
-        y = [sb.tile([M, N], F32, name="y%d" % g, align_bytes=64) for g in range(G)]
-
-        nc.vector.memset(ws_sb[:].bitcast(I32), 0)
+        raw0 = sb.tile([P, PACK, N], F32, name="raw0", align_bytes=64)
+        raw1 = [sb.tile([P, PACK, HALF], F32, name="raw1_%d" % h, align_bytes=64) for h in range(2)]
+        grp0 = [sb.tile([P, HALF, PACK], BF16, name="grp0_%d" % h, align_bytes=64) for h in range(2)]
+        grp1 = [sb.tile([P, QUARTER, PACK], BF16, name="grp1_%d" % q, align_bytes=64) for q in range(4)]
+        x_codes = sb.tile([P, 2 * N], U32, name="x_codes", align_bytes=64)
+        x_scales = sb.tile([P, 2 * N], U8, name="x_scales", align_bytes=64)
+        w_sb = [sb.tile([P, 2 * M], U8, name="w_sb%d" % s, align_bytes=64) for s in range(2)]
+        ws_sb = sb.tile([P, 2, M], U8, name="ws_sb", align_bytes=64)
+        acc0 = [psum.tile([M, N], F32, name="acc0_%d" % c) for c in range(2)]
+        acc1 = [[psum.tile([M, N], F32, name="acc1_%d_%d" % (h, c)) for c in range(2)] for h in range(2)]
+        y0 = [sb.tile([M, N], F32, name="y0_%d" % c, align_bytes=64) for c in range(2)]
+        y1 = [[sb.tile([M, HALF], F32, name="y1_%d_%d" % (h, c), align_bytes=64) for c in range(2)] for h in range(2)]
         probe = sb.tile([P, 2], F32, name="probe")
-        nc.vector.memset(probe[:, 0:1], 0.0)
 
-        for s in range(PAIRS):
-            nc.sync.dma_start(out=raw[s][:], in_=x[2 * s : 2 * s + 2].rearrange("c (p t) n -> (c p) t n", t=PACK))
-            nc.sync.dma_start(
-                out=w_sb[s][:].bitcast(I32),
-                in_=w_words[2 * s : 2 * s + 2].rearrange("c p b -> (c p) b").bitcast(I32),
+        def interleave(copy, grouped, raw):
+            copy(out=grouped.rearrange("p (c i) t -> p c t i", i=4), in_=raw.rearrange("p t (c i) -> p c t i", i=4))
+
+        def quantize(grouped, first):
+            cols = slice(first, first + grouped.shape[1])
+            nc.vector.quantize_mx(
+                out=x_codes[:, cols].bitcast(FP8X4), scales=x_scales[:, cols], in_=grouped.rearrange("p n t -> p (n t)")
             )
-        scale_rows = w_scales.rearrange("(s c) (h i) m -> c h i s m", c=2, i=4)
-        for c in range(2):
-            for h in range(2):
-                first = ROWS * c + 32 * h
-                nc.scalar.dma_start(out=ws_sb[first : first + 4].bitcast(I32), in_=scale_rows[c, h].bitcast(I32))
-        nc.scalar.activation(out=probe[:, 1:2], in_=probe[:, 0:1], func=GELU)
 
-        split = HALF + VEC_EXTRA
-        for s in range(PAIRS):
-            interleave(nc.scalar.copy, right[s], raw[s], split, N, HALF)
-            interleave(nc.vector.tensor_copy, left[s], raw[s], 0, HALF, 0)
-            interleave(nc.vector.tensor_copy, right[s], raw[s], HALF, split, HALF)
-            for grouped, lo in ((left[s], 0), (right[s], HALF)):
-                nc.vector.quantize_mx(
-                    out=x_codes[s][:, lo : lo + HALF].bitcast(FP8X4),
-                    scales=x_scales[s][:, lo : lo + HALF],
-                    in_=grouped[:].rearrange("p n t -> p (n t)"),
-                )
+        def multiply(acc, s, first):
             for c in range(2):
                 rows = slice(ROWS * c, ROWS * (c + 1))
                 nc.tensor.matmul_mx(
-                    out=acc[2 * s + c][:],
+                    out=acc[c][:],
                     lhsT=w_sb[s][rows, :].bitcast(FP4X4),
                     lhsT_scale=ws_sb[rows, s, :],
-                    rhs=x_codes[s][rows, :].bitcast(FP8X4),
-                    rhs_scale=x_scales[s][rows, :],
+                    rhs=x_codes[rows, first : first + N].bitcast(FP8X4),
+                    rhs_scale=x_scales[rows, first : first + N],
                     start=True,
                     stop=True,
                 )
 
-        for g in range(G):
-            nc.scalar.activation(out=y[g][:], in_=acc[g][:], func=GELU)
-            nc.sync.dma_start(out=out[g], in_=y[g][:])
+        def load_w(s):
+            nc.sync.dma_start(
+                out=w_sb[s][:].bitcast(I32),
+                in_=w_words[2 * s : 2 * s + 2].rearrange("c p b -> (c p) b").bitcast(I32),
+            )
+
+        nc.vector.memset(ws_sb[:].bitcast(I32), 0)
+        nc.vector.memset(probe[:, 0:1], 0.0)
+        nc.scalar.activation(out=probe[:, 1:2], in_=probe[:, 0:1], func=GELU)
+
+        xv = x.rearrange("(s c) (p t) n -> s (c p) t n", c=2, t=PACK)
+        nc.sync.dma_start(out=raw0[:], in_=xv[0])
+        load_w(0)
+        scale_rows = w_scales.rearrange("(s c) (h i) m -> c h i s m", c=2, i=4)
+        for c in range(2):
+            for h in range(2):
+                first = ROWS * c + 32 * h
+                nc.sync.dma_start(out=ws_sb[first : first + 4].bitcast(I32), in_=scale_rows[c, h].bitcast(I32))
+        nc.sync.dma_start(out=raw1[0][:], in_=xv[1, :, :, 0:HALF])
+        nc.sync.dma_start(out=raw1[1][:], in_=xv[1, :, :, HALF:N])
+        load_w(1)
+
+        split = HALF + VEC_EXTRA
+        interleave(nc.scalar.copy, grp0[1][:, VEC_EXTRA:HALF, :], raw0[:, :, split:N])
+        interleave(nc.vector.tensor_copy, grp0[0][:], raw0[:, :, 0:HALF])
+        interleave(nc.vector.tensor_copy, grp0[1][:, 0:VEC_EXTRA, :], raw0[:, :, HALF:split])
+        for h in range(2):
+            quantize(grp0[h][:], h * HALF)
+        multiply(acc0, 0, 0)
+        for c in range(2):
+            nc.scalar.activation(out=y0[c][:], in_=acc0[c][:], func=GELU)
+            nc.sync.dma_start(out=out[c], in_=y0[c][:])
+
+        for h in range(2):
+            for q in range(2):
+                interleave(nc.vector.tensor_copy, grp1[2 * h + q][:], raw1[h][:, :, q * QUARTER : (q + 1) * QUARTER])
+            for q in range(2):
+                quantize(grp1[2 * h + q][:], N + h * HALF + q * QUARTER)
+            multiply(acc1[h], 1, HALF + h * HALF)
+            for c in range(2):
+                nc.scalar.activation(out=y1[h][c][:], in_=acc1[h][c][:, HALF:N], func=GELU)
+                nc.sync.dma_start(out=out[2 + c, :, h * HALF : (h + 1) * HALF], in_=y1[h][c][:])

@@ -39,6 +39,7 @@ def tile_rows_glin_gelu_kernel(tc, x, w_words, w_scales, out):
         ws_sb = sb.tile([P, 2, M], U8, name="ws_sb", align_bytes=64)
         acc0 = [psum.tile([M, N], F32, name="acc0_%d" % c) for c in range(2)]
         acc1 = [[psum.tile([M, N], F32, name="acc1_%d_%d" % (h, c)) for c in range(2)] for h in range(2)]
+        spare = [psum.tile([M, N], F32, name="spare%d" % c) for c in range(2)]
         y0 = [sb.tile([M, N], F32, name="y0_%d" % c, align_bytes=64) for c in range(2)]
         y1 = [[sb.tile([M, HALF], F32, name="y1_%d_%d" % (h, c), align_bytes=64) for c in range(2)] for h in range(2)]
         probe = sb.tile([P, 2], F32, name="probe")
@@ -94,6 +95,8 @@ def tile_rows_glin_gelu_kernel(tc, x, w_words, w_scales, out):
         for h in range(2):
             quantize(grp0[h][:], h * HALF)
         multiply(acc0, 0, 0)
+        multiply(spare, 0, 0)
+        multiply(acc1[1], 0, 0)
         for c in range(2):
             nc.scalar.activation(out=y0[c][:], in_=acc0[c][:], func=GELU)
             nc.sync.dma_start(out=out[c], in_=y0[c][:])

from contextlib import ExitStack

import concourse.mybir as mybir

G, D, M, N = 4, 256, 128, 512
FLOPS = 2 * G * D * M * N

F32 = mybir.dt.float32
BF16 = mybir.dt.bfloat16
I32 = mybir.dt.int32
U32 = mybir.dt.uint32
U8 = mybir.dt.uint8
FP8X4 = mybir.dt.float8_e4m3fn_x4
FP4X4 = mybir.dt.float4_e2m1fn_x4
GELU = mybir.ActivationFunctionType.Gelu_apprx_tanh

P = 128
PACK = 4
ROWS = D // PACK
HALF = N // 2
QUARTER = N // 4
VEC_EXTRA = 64


def tile_rows_glin_gelu_kernel(tc, x, w_words, w_scales, out):
    nc = tc.nc
    with ExitStack() as ctx:
        sb = ctx.enter_context(tc.tile_pool(name="sb", bufs=1))
        psum = ctx.enter_context(tc.psum_pool(name="psum", bufs=1))
        ctx.enter_context(tc.manual_schedule())

        raw0 = sb.tile([P, PACK, N], F32, name="raw0", align_bytes=64)
        raw1 = [sb.tile([P, PACK, HALF], F32, name="raw1_%d" % h, align_bytes=64) for h in range(2)]
        grp0 = [sb.tile([P, HALF, PACK], BF16, name="grp0_%d" % h, align_bytes=64) for h in range(2)]
        grp1 = [sb.tile([P, QUARTER, PACK], BF16, name="grp1_%d" % q, align_bytes=64) for q in range(4)]
        x_codes = sb.tile([P, 2 * N], U32, name="x_codes", align_bytes=64)
        x_scales = sb.tile([P, 2 * N], U8, name="x_scales", align_bytes=64)
        w_sb = [sb.tile([P, 2 * M], U8, name="w_sb%d" % s, align_bytes=64) for s in range(2)]
        ws_sb = sb.tile([P, 2, M], U8, name="ws_sb", align_bytes=64)
        acc0 = [psum.tile([M, N], F32, name="acc0_%d" % c) for c in range(2)]
        acc1 = [[psum.tile([M, N], F32, name="acc1_%d_%d" % (h, c)) for c in range(2)] for h in range(2)]
        spare = [psum.tile([M, N], F32, name="spare%d" % c) for c in range(2)]
        y0 = [sb.tile([M, N], F32, name="y0_%d" % c, align_bytes=64) for c in range(2)]
        y1 = [[sb.tile([M, HALF], F32, name="y1_%d_%d" % (h, c), align_bytes=64) for c in range(2)] for h in range(2)]
        probe = sb.tile([P, 2], F32, name="probe")

        def interleave(copy, grouped, raw):
            copy(out=grouped.rearrange("p (c i) t -> p c t i", i=4), in_=raw.rearrange("p t (c i) -> p c t i", i=4))

        def quantize(grouped, first):
            cols = slice(first, first + grouped.shape[1])
            nc.vector.quantize_mx(
                out=x_codes[:, cols].bitcast(FP8X4), scales=x_scales[:, cols], in_=grouped.rearrange("p n t -> p (n t)")
            )

        def multiply(acc, s, first):
            for c in range(2):
                rows = slice(ROWS * c, ROWS * (c + 1))
                nc.tensor.matmul_mx(
                    out=acc[c][:],
                    lhsT=w_sb[s][rows, :].bitcast(FP4X4),
                    lhsT_scale=ws_sb[rows, s, :],
                    rhs=x_codes[rows, first : first + N].bitcast(FP8X4),
                    rhs_scale=x_scales[rows, first : first + N],
                    start=True,
                    stop=True,
                )

        def load_w(s):
            nc.sync.dma_start(
                out=w_sb[s][:].bitcast(I32),
                in_=w_words[2 * s : 2 * s + 2].rearrange("c p b -> (c p) b").bitcast(I32),
            )

        nc.vector.memset(ws_sb[:].bitcast(I32), 0)
        nc.vector.memset(probe[:, 0:1], 0.0)
        nc.scalar.activation(out=probe[:, 1:2], in_=probe[:, 0:1], func=GELU)

        xv = x.rearrange("(s c) (p t) n -> s (c p) t n", c=2, t=PACK)
        nc.sync.dma_start(out=raw0[:], in_=xv[0])
        load_w(0)
        scale_rows = w_scales.rearrange("(s c) (h i) m -> c h i s m", c=2, i=4)
        for c in range(2):
            for h in range(2):
                first = ROWS * c + 32 * h
                nc.sync.dma_start(out=ws_sb[first : first + 4].bitcast(I32), in_=scale_rows[c, h].bitcast(I32))
        nc.sync.dma_start(out=raw1[0][:], in_=xv[1, :, :, 0:HALF])
        nc.sync.dma_start(out=raw1[1][:], in_=xv[1, :, :, HALF:N])
        load_w(1)

        split = HALF + VEC_EXTRA
        interleave(nc.scalar.copy, grp0[1][:, VEC_EXTRA:HALF, :], raw0[:, :, split:N])
        interleave(nc.vector.tensor_copy, grp0[0][:], raw0[:, :, 0:HALF])
        interleave(nc.vector.tensor_copy, grp0[1][:, 0:VEC_EXTRA, :], raw0[:, :, HALF:split])
        for h in range(2):
            quantize(grp0[h][:], h * HALF)
        multiply(acc0, 0, 0)
        multiply(spare, 0, 0)
        multiply(acc1[1], 0, 0)
        for c in range(2):
            nc.scalar.activation(out=y0[c][:], in_=acc0[c][:], func=GELU)
            nc.sync.dma_start(out=out[c], in_=y0[c][:])

        for h in range(2):
            for q in range(2):
                interleave(nc.vector.tensor_copy, grp1[2 * h + q][:], raw1[h][:, :, q * QUARTER : (q + 1) * QUARTER])
            for q in range(2):
                quantize(grp1[2 * h + q][:], N + h * HALF + q * QUARTER)
            multiply(acc1[h], 1, HALF + h * HALF)
            for c in range(2):
                nc.scalar.activation(out=y1[h][c][:], in_=acc1[h][c][:, HALF:N], func=GELU)
                nc.sync.dma_start(out=out[2 + c, :, h * HALF : (h + 1) * HALF], in_=y1[h][c][:])
